import numpy as np, ml_dtypes
CORES = [26,28,98,100,106,108,122,124]
N = 8
KB, QP = 4, 64
WB = 1
def setup_inputs(rng):
    q = rng.standard_normal((N, 128, QP), dtype=np.float32) / 4; k = rng.standard_normal((N, 128, KB * 128), dtype=np.float32)
    a = 2 * np.pi * rng.random((N, QP)); s = 400 * rng.random((N, QP)) ** 1.5; q[:, 0, :] = s * np.cos(a); q[:, 1, :] = s * np.sin(a); q[:, 2, :] = 150 * rng.standard_normal((N, QP)); k[:, 2, :] = 1 + k[:, 2, :] / 50
    a = (2 * np.pi * rng.random() + np.pi / 2 * (rng.permutation(N).reshape(N, 1, 1) + 0.5) / N - 0.5 + (np.arange(KB).reshape(1, KB, 1) + rng.random((N, KB, 128))) / KB).reshape(N, KB * 128); k[:, 0, :] = np.cos(a); k[:, 1, :] = np.sin(a)
    return {"q": q.astype(ml_dtypes.bfloat16), "k": k.astype(ml_dtypes.bfloat16), "v": rng.standard_normal((N, 128, KB * 128), dtype=np.float32).astype(ml_dtypes.bfloat16)}
def setup_inputs_big(rng):
    d = setup_inputs(rng)
    for k in ("v",): d[k] = (d[k].astype(np.float32) * 1048576.0).astype(d[k].dtype)
    return d
def setup_inputs_small(rng):
    d = setup_inputs(rng)
    for k in ("v",): d[k] = (d[k].astype(np.float32) * (1 / 1048576.0)).astype(d[k].dtype)
    return d
def reference(q, k, v):
    Q, K, V = q.astype(np.float64), k.astype(np.float64), v.astype(np.float64)
    y = np.zeros((N, QP, 128))
    for r in range(N):
        js = list(range(max(0, r - WB), r + 1))
        S = np.concatenate([K[j].T @ Q[r] for j in js], axis=0)
        P = np.exp(S - S.max(axis=0)); P = P / P.sum(axis=0)
        y[r] = P.T @ np.concatenate([V[j][:, 128 * b:128 * b + 128] for j in js for b in range(KB)], axis=0)
    return {"y": y.astype(ml_dtypes.bfloat16)}

@@ -1,0 +1,233 @@
+from concourse.mybir import AluOpType, AxisListType, ActivationFunctionType
+
+QP, KB = 64, 4
+NE = 8
+MW = QP + 2
+
+SCRATCH = {
+    "qs": ("sbuf", [128, QP], "bfloat16"),
+    "ks": ("sbuf", [128, KB * 128], "bfloat16"),
+    "vs": ("sbuf", [128, KB * 128], "bfloat16"),
+    "qr": ("sbuf", [128, QP], "bfloat16"),
+    "dif": ("sbuf", [128, 128], "float32"),
+    "sqr": ("sbuf", [128, 128], "float32"),
+    "idn": ("sbuf", [128, 128], "bfloat16"),
+    "pta": ("sbuf", [128, KB * 128], "bfloat16"),
+    "pa": ("sbuf", [128, KB * QP], "bfloat16"),
+    "oa": ("sbuf", [128, 128], "bfloat16"),
+    "ptr": ("sbuf", [128, KB * 128], "bfloat16"),
+    "pr": ("sbuf", [128, KB * QP], "bfloat16"),
+    "msg": ("sbuf", [128, 72], "bfloat16"),
+    "land": ("sbuf", [128, 72], "bfloat16"),
+    "fwd": ("sbuf", [128, 72], "bfloat16"),
+    "col": ("sbuf", [128, 16], "float32"),
+    "dg": ("sbuf", [128, QP], "bfloat16"),
+    "ys": ("sbuf", [128, 128], "bfloat16"),
+    "b0": ("psum", [128, 512], "float32"),
+    "b1": ("psum", [128, 512], "float32"),
+    "b2": ("psum", [128, 512], "float32"),
+    "b3": ("psum", [128, 512], "float32"),
+    "bo": ("psum", [128, 512], "float32"),
+    "bl": ("psum", [128, 512], "float32"),
+    "bc": ("psum", [128, 512], "float32"),
+}
+SEMAPHORES = (["ldq", "ldk", "ldv", "sty", "qarr", "parr", "farr", "sent", "iod", "sqd", "idd", "msd",
+               "lsd", "lmd", "led", "ltd", "lcd", "lod", "locd", "rmd", "rgd", "rod", "rld", "rl2d", "rfd",
+               "cdd", "cbd", "ced", "cgd", "cmd", "cld", "crd", "cyd"]
+              + ["%s%d" % (s, c) for s in ("rs", "re", "rt", "rc") for c in range(KB)])
+
+
+def _engines(mask, n):
+    out, b = 0, 0
+    while n:
+        if (mask >> b) & 1:
+            out |= 1 << b
+            n -= 1
+        b += 1
+    return out
+
+
+def _relays(cores, topo):
+    relay, used = {}, []
+    for r in range(len(cores) - 1):
+        s, d = cores[r], cores[r + 1]
+        relay[r] = None
+        if topo.may_write(s, d):
+            continue
+        cand = [x for x in range(topo.CHIPS * topo.CORES_PER_CHIP)
+                if topo.chip(x) == topo.chip(s) and x != s and x not in used and topo.may_write(x, d)]
+        cand.sort(key=lambda x: (x not in cores, topo.die(x) != topo.die(d), x))
+        relay[r] = cand[0]
+        used.append(cand[0])
+    return relay
+
+
+def rank_program(g, core, T, topo):
+    cores = list(T.cores)
+    rank = T.rank_of(core)
+    relay = _relays(cores, topo)
+    duty = [r for r in relay if relay[r] == core]
+    if rank is None and not duty:
+        return
+    S = T.sem
+    sent = [0]
+
+    def send(dst, out_ap, in_ap, rsem):
+        rid, pid, _se = topo.addr(dst)
+        g.remote_dma(out_ap=out_ap, in_ap=in_ap, remote_sem=rsem, local_sem=S.sent, pid=pid, routing_id=rid,
+                     dma_engine_mask=_engines(topo.mask(core, dst), NE))
+        sent[0] += NE
+
+    def pass_on():
+        for r in duty:
+            g.wait_ge(S.farr, NE)
+            send(cores[r + 1], T.land[:, 0:MW], T.fwd[:, 0:MW], S.parr)
+        if sent[0]:
+            g.wait_ge(S.sent, sent[0])
+
+    if rank is None:
+        pass_on()
+        return
+
+    has_prev, has_next = rank > 0, rank < len(cores) - 1
+    pe, dve, act, sp = g.tensor, g.vector, g.scalar, g.sync
+    X, A, F = AxisListType.X, AluOpType, ActivationFunctionType
+    H = slice(0, QP)
+    na, la, lsum, dc, ec, lc, rc, lb = [T.col[H, i:i + 1] for i in range(8)]
+    mx, lp = T.col[H, 8:8 + KB], T.col[H, 12:12 + KB]
+    B = [T.b0, T.b1, T.b2, T.b3]
+
+    def kb(c):
+        return slice(128 * c, 128 * c + 128)
+
+    def qb(c):
+        return slice(QP * c, QP * c + QP)
+
+    sp.dma_start(T.qs[:], T.q[:]).then_inc(S.ldq, 16)
+    sp.dma_start(T.ks[:], T.k[:]).then_inc(S.ldk, 16)
+    sp.dma_start(T.vs[:], T.v[:]).then_inc(S.ldv, 16)
+
+    g.iota(T.dif[:], [[-1, 128]], 0, 1, allow_small_or_imprecise_dtypes=True).then_inc(S.iod, 1)
+    act.wait_ge(S.iod, 1)
+    act.activation(T.sqr[:], T.dif[:], F.Square).then_inc(S.sqd, 1)
+    act.wait_ge(S.sqd, 1)
+    act.activation(T.idn[:], T.sqr[:], F.Exp, scale=-100.0).then_inc(S.idd, 1)
+    if has_next:
+        dve.memset(T.msg[QP:128, QP:MW], 0.0).then_inc(S.msd, 1)
+
+    if has_prev:
+        g.wait_ge(S.ldq, 16)
+        send(cores[rank - 1], T.qr[:], T.qs[:], S.qarr)
+
+    pe.wait_ge(S.ldq, 16)
+    pe.wait_ge(S.ldk, 16)
+    pe.matmul(T.bl[H, :], T.qs[:], T.ks[:], start=True, stop=True).then_inc(S.lsd, 1)
+    dve.wait_ge(S.lsd, 1)
+    dve.tensor_reduce(na, T.bl[H, :], X, A.max, negate=True).then_inc(S.lmd, 1)
+    act.wait_ge(S.lmd, 1)
+    act.activation(T.pta[H, :], T.bl[H, :], F.Exp, bias=na, accum_out=la).then_inc(S.led, 1)
+    pe.wait_ge(S.idd, 1)
+
+    if has_next:
+        nm = T.msg[H, QP:QP + 1]
+        pe.wait_ge(S.qarr, NE)
+        for c in range(KB):
+            pe.matmul(B[c][H, 0:128], T.qr[:], T.ks[:, kb(c)], start=True, stop=True).then_inc(S["rs%d" % c], 1)
+        for c in range(KB):
+            dve.wait_ge(S["rs%d" % c], 1)
+            dve.tensor_reduce(T.col[H, 8 + c:9 + c], B[c][H, 0:128], X, A.max).then_inc(S.rmd, 1)
+        dve.wait_ge(S.rmd, KB)
+        dve.tensor_reduce(nm, mx, X, A.max, negate=True).then_inc(S.rgd, 1)
+        act.wait_ge(S.rgd, 1)
+        for c in range(KB):
+            act.activation(T.ptr[H, kb(c)], B[c][H, 0:128], F.Exp, bias=nm,
+                           accum_out=T.col[H, 12 + c:13 + c]).then_inc(S["re%d" % c], 1)
+
+        def turn(c):
+            pe.wait_ge(S["re%d" % c], 1)
+            pe.matmul(B[c][:, 128:128 + QP], T.ptr[H, kb(c)], T.idn[H, H], start=True, stop=True
+                      ).then_inc(S["rt%d" % c], 1)
+
+        def vsum(c):
+            pe.wait_ge(S["rc%d" % c], 1)
+            pe.matmul(T.bo[:, H], T.vs[:, kb(c)], T.pr[:, qb(c)], start=(c == 0), stop=(c == KB - 1)
+                      ).then_inc(S.rod, 1)
+
+        def down(c):
+            dve.wait_ge(S["rt%d" % c], 1)
+            dve.tensor_copy(T.pr[:, qb(c)], B[c][:, 128:128 + QP]).then_inc(S["rc%d" % c], 1)
+
+        turn(0)
+        turn(1)
+        pe.wait_ge(S.ldv, 16)
+        vsum(0)
+        turn(2)
+        vsum(1)
+        turn(3)
+        vsum(2)
+        vsum(3)
+        down(0)
+        down(1)
+        down(2)
+        for c in range(KB):
+            dve.wait_ge(S["re%d" % c], 1)
+        dve.tensor_reduce(lsum, lp, X, A.add).then_inc(S.rld, 1)
+        down(3)
+        dve.wait_ge(S.rld, 1)
+        dve.tensor_copy(T.msg[H, QP + 1:QP + 2], lsum).then_inc(S.rl2d, 1)
+        dve.wait_ge(S.rod, KB)
+        dve.tensor_copy(T.msg[:, H], T.bo[:, H]).then_inc(S.rfd, 1)
+
+        for s in (S.msd, S.rgd, S.rl2d, S.rfd):
+            g.wait_ge(s, 1)
+        if relay[rank] is None:
+            send(cores[rank + 1], T.land[:, 0:MW], T.msg[:, 0:MW], S.parr)
+        else:
+            send(relay[rank], T.fwd[:, 0:MW], T.msg[:, 0:MW], S.farr)
+    pass_on()
+
+    pe.wait_ge(S.led, 1)
+    for c in range(KB):
+        pe.matmul(T.bl[:, qb(c)], T.pta[H, kb(c)], T.idn[H, H], start=True, stop=True).then_inc(S.ltd, 1)
+    dve.wait_ge(S.ltd, KB)
+    dve.tensor_copy(T.pa[:], T.bl[:, 0:KB * QP]).then_inc(S.lcd, 1)
+    pe.wait_ge(S.lcd, 1)
+    pe.wait_ge(S.ldv, 16)
+    ob = T.bl[H, KB * QP:KB * QP + 128]
+    for c in range(KB):
+        pe.matmul(ob, T.pa[:, qb(c)], T.vs[:, kb(c)], start=(c == 0), stop=(c == KB - 1)).then_inc(S.lod, 1)
+    dve.wait_ge(S.lod, KB)
+    dve.wait_ge(S.led, 1)
+
+    if not has_prev:
+        dve.reciprocal(rc, la).then_inc(S.crd, 1)
+        dve.wait_ge(S.crd, 1)
+        dve.tensor_scalar(T.ys[H, :], ob, rc, None, A.mult).then_inc(S.cyd, 1)
+    else:
+        dve.tensor_copy(T.oa[H, :], ob).then_inc(S.locd, 1)
+        pe.wait_ge(S.parr, NE)
+        pe.matmul(T.bc[H, 0:128], T.land[:, H], T.idn[:], start=True, stop=False).then_inc(S.cmd, 1)
+        dve.wait_ge(S.parr, NE)
+        dve.wait_ge(S.lmd, 1)
+        dve.tensor_scalar(dc, T.land[H, QP:QP + 1], na, 60.0, A.subtract, A.min).then_inc(S.cdd, 1)
+        dve.tensor_copy(lb, T.land[H, QP + 1:QP + 2]).then_inc(S.cbd, 1)
+        act.wait_ge(S.cdd, 1)
+        act.activation(ec, dc, F.Exp).then_inc(S.ced, 1)
+        act.wait_ge(S.ced, 1)
+        act.wait_ge(S.idd, 1)
+        act.activation(T.dg[H, :], T.idn[H, H], F.Copy, scale=ec).then_inc(S.cgd, 1)
+        pe.wait_ge(S.cgd, 1)
+        pe.wait_ge(S.locd, 1)
+        pe.matmul(T.bc[H, 0:128], T.dg[H, :], T.oa[H, :], start=False, stop=True).then_inc(S.cmd, 1)
+        dve.wait_ge(S.ced, 1)
+        dve.wait_ge(S.cbd, 1)
+        dve.tensor_scalar(lc, la, ec, lb, A.mult, A.add).then_inc(S.cld, 1)
+        dve.wait_ge(S.cld, 1)
+        dve.reciprocal(rc, lc).then_inc(S.crd, 1)
+        dve.wait_ge(S.crd, 1)
+        dve.wait_ge(S.cmd, 2)
+        dve.tensor_scalar(T.ys[H, :], T.bc[H, 0:128], rc, None, A.mult).then_inc(S.cyd, 1)
+
+    sp.wait_ge(S.cyd, 1)
+    sp.dma_start(T.y[:], T.ys[H, :]).then_inc(S.sty, 16)
+    sp.wait_ge(S.sty, 16)

@@ -8,6 +8,8 @@ SCRATCH = {
     "qs": ("sbuf", [128, QP], "bfloat16"),
     "ks": ("sbuf", [128, KB * 128], "bfloat16"),
     "vs": ("sbuf", [128, KB * 128], "bfloat16"),
+    "kx": ("sbuf", [128, KB * 128], "bfloat16"),
+    "vx": ("sbuf", [128, KB * 128], "bfloat16"),
     "qr": ("sbuf", [128, QP], "bfloat16"),
     "dif": ("sbuf", [128, 128], "float32"),
     "sqr": ("sbuf", [128, 128], "float32"),
@@ -19,7 +21,6 @@ SCRATCH = {
     "pr": ("sbuf", [128, KB * QP], "bfloat16"),
     "msg": ("sbuf", [128, 72], "bfloat16"),
     "land": ("sbuf", [128, 72], "bfloat16"),
-    "fwd": ("sbuf", [128, 72], "bfloat16"),
     "col": ("sbuf", [128, 16], "float32"),
     "dg": ("sbuf", [128, QP], "bfloat16"),
     "ys": ("sbuf", [128, 128], "bfloat16"),
@@ -31,7 +32,7 @@ SCRATCH = {
     "bl": ("psum", [128, 512], "float32"),
     "bc": ("psum", [128, 512], "float32"),
 }
-SEMAPHORES = (["ldq", "ldk", "ldv", "sty", "qarr", "parr", "farr", "sent", "iod", "sqd", "idd", "msd",
+SEMAPHORES = (["ldq", "ldk", "ldv", "sty", "qarr", "parr", "kxa", "vxa", "sent", "iod", "sqd", "idd", "msd",
                "lsd", "lmd", "led", "ltd", "lcd", "lod", "locd", "rmd", "rgd", "rod", "rld", "rl2d", "rfd",
                "cdd", "cbd", "ced", "cgd", "cmd", "cld", "crd", "cyd"]
               + ["%s%d" % (s, c) for s in ("rs", "re", "rt", "rc") for c in range(KB)])
@@ -47,51 +48,52 @@ def _engines(mask, n):
     return out
 
 
-def _relays(cores, topo):
-    relay, used = {}, []
-    for r in range(len(cores) - 1):
-        s, d = cores[r], cores[r + 1]
-        relay[r] = None
-        if topo.may_write(s, d):
+def _plan(cores, topo):
+    X = {e: cores[e] for e in range(len(cores) - 1)}
+    pair = {}
+    for e in range(len(cores) - 1):
+        if topo.may_write(cores[e], cores[e + 1]):
             continue
-        cand = [x for x in range(topo.CHIPS * topo.CORES_PER_CHIP)
-                if topo.chip(x) == topo.chip(s) and x != s and x not in used and topo.may_write(x, d)]
-        cand.sort(key=lambda x: (x not in cores, topo.die(x) != topo.die(d), x))
-        relay[r] = cand[0]
-        used.append(cand[0])
-    return relay
+        p = cores[e - 1] if e else None
+        if p is None or topo.chip(p) != topo.chip(cores[e]) or not topo.may_write(p, cores[e + 1]):
+            raise ValueError("no rank on the holder's chip may write to the asker")
+        X[e], X[e - 1] = p, cores[e]
+        pair[p], pair[cores[e]] = cores[e], p
+    return X, pair
 
 
 def rank_program(g, core, T, topo):
     cores = list(T.cores)
     rank = T.rank_of(core)
-    relay = _relays(cores, topo)
-    duty = [r for r in relay if relay[r] == core]
-    if rank is None and not duty:
+    if rank is None:
         return
+    X, pair = _plan(cores, topo)
     S = T.sem
     sent = [0]
 
-    def send(dst, out_ap, in_ap, rsem):
+    def send(dst, out_ap, in_ap, rsem, wide=False):
         rid, pid, _se = topo.addr(dst)
+        m = topo.mask(core, dst)
+        if not wide:
+            m = _engines(m, NE)
         g.remote_dma(out_ap=out_ap, in_ap=in_ap, remote_sem=rsem, local_sem=S.sent, pid=pid, routing_id=rid,
-                     dma_engine_mask=_engines(topo.mask(core, dst), NE))
-        sent[0] += NE
+                     dma_engine_mask=m)
+        sent[0] += bin(m).count("1")
 
-    def pass_on():
-        for r in duty:
-            g.wait_ge(S.farr, NE)
-            send(cores[r + 1], T.land[:, 0:MW], T.fwd[:, 0:MW], S.parr)
-        if sent[0]:
-            g.wait_ge(S.sent, sent[0])
+    has_prev = rank > 0
+    mate = pair.get(core)
+    mine = [e for e in X if X[e] == core]
+    has_part = len(mine) > 0
+    edge = mine[0] if has_part else -1
+    own_q = has_part and cores[edge + 1] == core
+    own_kv = has_part and cores[edge] == core
+    asks = has_prev and X[rank - 1] != core
+    nw = bin(topo.mask(mate, core)).count("1") if mate is not None else 0
+    Rq = T.qs if own_q else T.qr
+    Rk, Rv = (T.ks, T.vs) if own_kv else (T.kx, T.vx)
 
-    if rank is None:
-        pass_on()
-        return
-
-    has_prev, has_next = rank > 0, rank < len(cores) - 1
     pe, dve, act, sp = g.tensor, g.vector, g.scalar, g.sync
-    X, A, F = AxisListType.X, AluOpType, ActivationFunctionType
+    X_, A, F = AxisListType.X, AluOpType, ActivationFunctionType
     H = slice(0, QP)
     na, la, lsum, dc, ec, lc, rc, lb = [T.col[H, i:i + 1] for i in range(8)]
     mx, lp = T.col[H, 8:8 + KB], T.col[H, 12:12 + KB]
@@ -103,41 +105,55 @@ def rank_program(g, core, T, topo):
     def qb(c):
         return slice(QP * c, QP * c + QP)
 
-    sp.dma_start(T.qs[:], T.q[:]).then_inc(S.ldq, 16)
+    def load_q():
+        sp.dma_start(T.qs[:], T.q[:]).then_inc(S.ldq, 16)
+
+    if asks:
+        load_q()
     sp.dma_start(T.ks[:], T.k[:]).then_inc(S.ldk, 16)
     sp.dma_start(T.vs[:], T.v[:]).then_inc(S.ldv, 16)
+    if not asks:
+        load_q()
 
     g.iota(T.dif[:], [[-1, 128]], 0, 1, allow_small_or_imprecise_dtypes=True).then_inc(S.iod, 1)
     act.wait_ge(S.iod, 1)
     act.activation(T.sqr[:], T.dif[:], F.Square).then_inc(S.sqd, 1)
     act.wait_ge(S.sqd, 1)
     act.activation(T.idn[:], T.sqr[:], F.Exp, scale=-100.0).then_inc(S.idd, 1)
-    if has_next:
+    if has_part and not own_q:
         dve.memset(T.msg[QP:128, QP:MW], 0.0).then_inc(S.msd, 1)
 
-    if has_prev:
+    if asks:
         g.wait_ge(S.ldq, 16)
-        send(cores[rank - 1], T.qr[:], T.qs[:], S.qarr)
+        send(X[rank - 1], T.qr[:], T.qs[:], S.qarr)
+    if mate is not None:
+        g.wait_ge(S.ldk, 16)
+        send(mate, T.kx[:], T.ks[:], S.kxa, wide=True)
+        g.wait_ge(S.ldv, 16)
+        send(mate, T.vx[:], T.vs[:], S.vxa, wide=True)
 
     pe.wait_ge(S.ldq, 16)
     pe.wait_ge(S.ldk, 16)
     pe.matmul(T.bl[H, :], T.qs[:], T.ks[:], start=True, stop=True).then_inc(S.lsd, 1)
     dve.wait_ge(S.lsd, 1)
-    dve.tensor_reduce(na, T.bl[H, :], X, A.max, negate=True).then_inc(S.lmd, 1)
+    dve.tensor_reduce(na, T.bl[H, :], X_, A.max, negate=True).then_inc(S.lmd, 1)
     act.wait_ge(S.lmd, 1)
     act.activation(T.pta[H, :], T.bl[H, :], F.Exp, bias=na, accum_out=la).then_inc(S.led, 1)
     pe.wait_ge(S.idd, 1)
 
-    if has_next:
+    if has_part:
         nm = T.msg[H, QP:QP + 1]
-        pe.wait_ge(S.qarr, NE)
+        if not own_q:
+            pe.wait_ge(S.qarr, NE)
+        if not own_kv:
+            pe.wait_ge(S.kxa, nw)
         for c in range(KB):
-            pe.matmul(B[c][H, 0:128], T.qr[:], T.ks[:, kb(c)], start=True, stop=True).then_inc(S["rs%d" % c], 1)
+            pe.matmul(B[c][H, 0:128], Rq[:], Rk[:, kb(c)], start=True, stop=True).then_inc(S["rs%d" % c], 1)
         for c in range(KB):
             dve.wait_ge(S["rs%d" % c], 1)
-            dve.tensor_reduce(T.col[H, 8 + c:9 + c], B[c][H, 0:128], X, A.max).then_inc(S.rmd, 1)
+            dve.tensor_reduce(T.col[H, 8 + c:9 + c], B[c][H, 0:128], X_, A.max).then_inc(S.rmd, 1)
         dve.wait_ge(S.rmd, KB)
-        dve.tensor_reduce(nm, mx, X, A.max, negate=True).then_inc(S.rgd, 1)
+        dve.tensor_reduce(nm, mx, X_, A.max, negate=True).then_inc(S.rgd, 1)
         act.wait_ge(S.rgd, 1)
         for c in range(KB):
             act.activation(T.ptr[H, kb(c)], B[c][H, 0:128], F.Exp, bias=nm,
@@ -150,7 +166,7 @@ def rank_program(g, core, T, topo):
 
         def vsum(c):
             pe.wait_ge(S["rc%d" % c], 1)
-            pe.matmul(T.bo[:, H], T.vs[:, kb(c)], T.pr[:, qb(c)], start=(c == 0), stop=(c == KB - 1)
+            pe.matmul(T.bo[:, H], Rv[:, kb(c)], T.pr[:, qb(c)], start=(c == 0), stop=(c == KB - 1)
                       ).then_inc(S.rod, 1)
 
         def down(c):
@@ -159,7 +175,10 @@ def rank_program(g, core, T, topo):
 
         turn(0)
         turn(1)
-        pe.wait_ge(S.ldv, 16)
+        if own_kv:
+            pe.wait_ge(S.ldv, 16)
+        else:
+            pe.wait_ge(S.vxa, nw)
         vsum(0)
         turn(2)
         vsum(1)
@@ -171,20 +190,19 @@ def rank_program(g, core, T, topo):
         down(2)
         for c in range(KB):
             dve.wait_ge(S["re%d" % c], 1)
-        dve.tensor_reduce(lsum, lp, X, A.add).then_inc(S.rld, 1)
+        dve.tensor_reduce(lsum, lp, X_, A.add).then_inc(S.rld, 1)
         down(3)
         dve.wait_ge(S.rld, 1)
         dve.tensor_copy(T.msg[H, QP + 1:QP + 2], lsum).then_inc(S.rl2d, 1)
         dve.wait_ge(S.rod, KB)
         dve.tensor_copy(T.msg[:, H], T.bo[:, H]).then_inc(S.rfd, 1)
 
-        for s in (S.msd, S.rgd, S.rl2d, S.rfd):
-            g.wait_ge(s, 1)
-        if relay[rank] is None:
-            send(cores[rank + 1], T.land[:, 0:MW], T.msg[:, 0:MW], S.parr)
-        else:
-            send(relay[rank], T.fwd[:, 0:MW], T.msg[:, 0:MW], S.farr)
-    pass_on()
+        if not own_q:
+            for s in (S.msd, S.rgd, S.rl2d, S.rfd):
+                g.wait_ge(s, 1)
+            send(cores[edge + 1], T.land[:, 0:MW], T.msg[:, 0:MW], S.parr)
+    if sent[0]:
+        g.wait_ge(S.sent, sent[0])
 
     pe.wait_ge(S.led, 1)
     for c in range(KB):
@@ -202,15 +220,25 @@ def rank_program(g, core, T, topo):
     if not has_prev:
         dve.reciprocal(rc, la).then_inc(S.crd, 1)
         dve.wait_ge(S.crd, 1)
-        dve.tensor_scalar(T.ys[H, :], ob, rc, None, A.mult).then_inc(S.cyd, 1)
+        dve.tensor_scalar(T.ys[H, :], ob, rc, None, A.mult).then_inc(S.cyd, 2)
     else:
         dve.tensor_copy(T.oa[H, :], ob).then_inc(S.locd, 1)
-        pe.wait_ge(S.parr, NE)
-        pe.matmul(T.bc[H, 0:128], T.land[:, H], T.idn[:], start=True, stop=False).then_inc(S.cmd, 1)
-        dve.wait_ge(S.parr, NE)
+        part = T.land if asks else T.msg
+
+        def there(qu):
+            if asks:
+                qu.wait_ge(S.parr, NE)
+            else:
+                for s in (S.rgd, S.rl2d, S.rfd):
+                    qu.wait_ge(s, 1)
+
+        there(pe)
+        pe.matmul(T.bc[H, H], part[:, H], T.idn[:, 0:QP], start=True, stop=False).then_inc(S.cmd, 1)
+        pe.matmul(T.b0[H, H], part[:, H], T.idn[:, QP:128], start=True, stop=False).then_inc(S.cmd, 1)
+        there(dve)
         dve.wait_ge(S.lmd, 1)
-        dve.tensor_scalar(dc, T.land[H, QP:QP + 1], na, 60.0, A.subtract, A.min).then_inc(S.cdd, 1)
-        dve.tensor_copy(lb, T.land[H, QP + 1:QP + 2]).then_inc(S.cbd, 1)
+        dve.tensor_scalar(dc, part[H, QP:QP + 1], na, 60.0, A.subtract, A.min).then_inc(S.cdd, 1)
+        dve.tensor_copy(lb, part[H, QP + 1:QP + 2]).then_inc(S.cbd, 1)
         act.wait_ge(S.cdd, 1)
         act.activation(ec, dc, F.Exp).then_inc(S.ced, 1)
         act.wait_ge(S.ced, 1)
@@ -218,16 +246,20 @@ def rank_program(g, core, T, topo):
         act.activation(T.dg[H, :], T.idn[H, H], F.Copy, scale=ec).then_inc(S.cgd, 1)
         pe.wait_ge(S.cgd, 1)
         pe.wait_ge(S.locd, 1)
-        pe.matmul(T.bc[H, 0:128], T.dg[H, :], T.oa[H, :], start=False, stop=True).then_inc(S.cmd, 1)
+        pe.matmul(T.bc[H, H], T.dg[H, :], T.oa[H, 0:QP], start=False, stop=True).then_inc(S.cmd, 1)
+        pe.matmul(T.b0[H, H], T.dg[H, :], T.oa[H, QP:128], start=False, stop=True).then_inc(S.cmd, 1)
         dve.wait_ge(S.ced, 1)
         dve.wait_ge(S.cbd, 1)
         dve.tensor_scalar(lc, la, ec, lb, A.mult, A.add).then_inc(S.cld, 1)
         dve.wait_ge(S.cld, 1)
         dve.reciprocal(rc, lc).then_inc(S.crd, 1)
         dve.wait_ge(S.crd, 1)
-        dve.wait_ge(S.cmd, 2)
-        dve.tensor_scalar(T.ys[H, :], T.bc[H, 0:128], rc, None, A.mult).then_inc(S.cyd, 1)
+        dve.wait_ge(S.cmd, 4)
+        dve.tensor_scalar(T.ys[H, 0:QP], T.bc[H, H], rc, None, A.mult).then_inc(S.cyd, 1)
+        act.wait_ge(S.crd, 1)
+        act.wait_ge(S.cmd, 4)
+        act.activation(T.ys[H, QP:128], T.b0[H, H], F.Copy, scale=rc).then_inc(S.cyd, 1)
 
-    sp.wait_ge(S.cyd, 1)
+    sp.wait_ge(S.cyd, 2)
     sp.dma_start(T.y[:], T.ys[H, :]).then_inc(S.sty, 16)
     sp.wait_ge(S.sty, 16)

from concourse.mybir import AluOpType, AxisListType, ActivationFunctionType

QP, KB = 64, 4
NE = 8
MW = QP + 2

SCRATCH = {
    "qs": ("sbuf", [128, QP], "bfloat16"),
    "ks": ("sbuf", [128, KB * 128], "bfloat16"),
    "vs": ("sbuf", [128, KB * 128], "bfloat16"),
    "kx": ("sbuf", [128, KB * 128], "bfloat16"),
    "vx": ("sbuf", [128, KB * 128], "bfloat16"),
    "qr": ("sbuf", [128, QP], "bfloat16"),
    "dif": ("sbuf", [128, 128], "float32"),
    "sqr": ("sbuf", [128, 128], "float32"),
    "idn": ("sbuf", [128, 128], "bfloat16"),
    "pta": ("sbuf", [128, KB * 128], "bfloat16"),
    "pa": ("sbuf", [128, KB * QP], "bfloat16"),
    "oa": ("sbuf", [128, 128], "bfloat16"),
    "ptr": ("sbuf", [128, KB * 128], "bfloat16"),
    "pr": ("sbuf", [128, KB * QP], "bfloat16"),
    "msg": ("sbuf", [128, 72], "bfloat16"),
    "land": ("sbuf", [128, 72], "bfloat16"),
    "col": ("sbuf", [128, 16], "float32"),
    "dg": ("sbuf", [128, QP], "bfloat16"),
    "ys": ("sbuf", [128, 128], "bfloat16"),
    "b0": ("psum", [128, 512], "float32"),
    "b1": ("psum", [128, 512], "float32"),
    "b2": ("psum", [128, 512], "float32"),
    "b3": ("psum", [128, 512], "float32"),
    "bo": ("psum", [128, 512], "float32"),
    "bl": ("psum", [128, 512], "float32"),
    "bc": ("psum", [128, 512], "float32"),
}
SEMAPHORES = (["ldq", "ldk", "ldv", "sty", "qarr", "parr", "kxa", "vxa", "sent", "iod", "sqd", "idd", "msd",
               "lsd", "lmd", "led", "ltd", "lcd", "lod", "locd", "rmd", "rgd", "rod", "rld", "rl2d", "rfd",
               "cdd", "cbd", "ced", "cgd", "cmd", "cld", "crd", "cyd"]
              + ["%s%d" % (s, c) for s in ("rs", "re", "rt", "rc") for c in range(KB)])


def _engines(mask, n):
    out, b = 0, 0
    while n:
        if (mask >> b) & 1:
            out |= 1 << b
            n -= 1
        b += 1
    return out


def _plan(cores, topo):
    X = {e: cores[e] for e in range(len(cores) - 1)}
    pair = {}
    for e in range(len(cores) - 1):
        if topo.may_write(cores[e], cores[e + 1]):
            continue
        p = cores[e - 1] if e else None
        if p is None or topo.chip(p) != topo.chip(cores[e]) or not topo.may_write(p, cores[e + 1]):
            raise ValueError("no rank on the holder's chip may write to the asker")
        X[e], X[e - 1] = p, cores[e]
        pair[p], pair[cores[e]] = cores[e], p
    return X, pair


def rank_program(g, core, T, topo):
    cores = list(T.cores)
    rank = T.rank_of(core)
    if rank is None:
        return
    X, pair = _plan(cores, topo)
    S = T.sem
    sent = [0]

    def send(dst, out_ap, in_ap, rsem, wide=False):
        rid, pid, _se = topo.addr(dst)
        m = topo.mask(core, dst)
        if not wide:
            m = _engines(m, NE)
        g.remote_dma(out_ap=out_ap, in_ap=in_ap, remote_sem=rsem, local_sem=S.sent, pid=pid, routing_id=rid,
                     dma_engine_mask=m)
        sent[0] += bin(m).count("1")

    has_prev = rank > 0
    mate = pair.get(core)
    mine = [e for e in X if X[e] == core]
    has_part = len(mine) > 0
    edge = mine[0] if has_part else -1
    own_q = has_part and cores[edge + 1] == core
    own_kv = has_part and cores[edge] == core
    asks = has_prev and X[rank - 1] != core
    nw = bin(topo.mask(mate, core)).count("1") if mate is not None else 0
    Rq = T.qs if own_q else T.qr
    Rk, Rv = (T.ks, T.vs) if own_kv else (T.kx, T.vx)

    pe, dve, act, sp = g.tensor, g.vector, g.scalar, g.sync
    X_, A, F = AxisListType.X, AluOpType, ActivationFunctionType
    H = slice(0, QP)
    na, la, lsum, dc, ec, lc, rc, lb = [T.col[H, i:i + 1] for i in range(8)]
    mx, lp = T.col[H, 8:8 + KB], T.col[H, 12:12 + KB]
    B = [T.b0, T.b1, T.b2, T.b3]

    def kb(c):
        return slice(128 * c, 128 * c + 128)

    def qb(c):
        return slice(QP * c, QP * c + QP)

    def load_q():
        sp.dma_start(T.qs[:], T.q[:]).then_inc(S.ldq, 16)

    if asks:
        load_q()
    sp.dma_start(T.ks[:], T.k[:]).then_inc(S.ldk, 16)
    sp.dma_start(T.vs[:], T.v[:]).then_inc(S.ldv, 16)
    if not asks:
        load_q()

    g.iota(T.dif[:], [[-1, 128]], 0, 1, allow_small_or_imprecise_dtypes=True).then_inc(S.iod, 1)
    act.wait_ge(S.iod, 1)
    act.activation(T.sqr[:], T.dif[:], F.Square).then_inc(S.sqd, 1)
    act.wait_ge(S.sqd, 1)
    act.activation(T.idn[:], T.sqr[:], F.Exp, scale=-100.0).then_inc(S.idd, 1)
    if has_part and not own_q:
        dve.memset(T.msg[QP:128, QP:MW], 0.0).then_inc(S.msd, 1)

    if asks:
        g.wait_ge(S.ldq, 16)
        send(X[rank - 1], T.qr[:], T.qs[:], S.qarr)
    if mate is not None:
        g.wait_ge(S.ldk, 16)
        send(mate, T.kx[:], T.ks[:], S.kxa, wide=True)
        g.wait_ge(S.ldv, 16)
        send(mate, T.vx[:], T.vs[:], S.vxa, wide=True)

    pe.wait_ge(S.ldq, 16)
    pe.wait_ge(S.ldk, 16)
    pe.matmul(T.bl[H, :], T.qs[:], T.ks[:], start=True, stop=True).then_inc(S.lsd, 1)
    dve.wait_ge(S.lsd, 1)
    dve.tensor_reduce(na, T.bl[H, :], X_, A.max, negate=True).then_inc(S.lmd, 1)
    act.wait_ge(S.lmd, 1)
    act.activation(T.pta[H, :], T.bl[H, :], F.Exp, bias=na, accum_out=la).then_inc(S.led, 1)
    pe.wait_ge(S.idd, 1)

    if has_part:
        nm = T.msg[H, QP:QP + 1]
        if not own_q:
            pe.wait_ge(S.qarr, NE)
        if not own_kv:
            pe.wait_ge(S.kxa, nw)
        for c in range(KB):
            pe.matmul(B[c][H, 0:128], Rq[:], Rk[:, kb(c)], start=True, stop=True).then_inc(S["rs%d" % c], 1)
        for c in range(KB):
            dve.wait_ge(S["rs%d" % c], 1)
            dve.tensor_reduce(T.col[H, 8 + c:9 + c], B[c][H, 0:128], X_, A.max).then_inc(S.rmd, 1)
        dve.wait_ge(S.rmd, KB)
        dve.tensor_reduce(nm, mx, X_, A.max, negate=True).then_inc(S.rgd, 1)
        act.wait_ge(S.rgd, 1)
        for c in range(KB):
            act.activation(T.ptr[H, kb(c)], B[c][H, 0:128], F.Exp, bias=nm,
                           accum_out=T.col[H, 12 + c:13 + c]).then_inc(S["re%d" % c], 1)

        def turn(c):
            pe.wait_ge(S["re%d" % c], 1)
            pe.matmul(B[c][:, 128:128 + QP], T.ptr[H, kb(c)], T.idn[H, H], start=True, stop=True
                      ).then_inc(S["rt%d" % c], 1)

        def vsum(c):
            pe.wait_ge(S["rc%d" % c], 1)
            pe.matmul(T.bo[:, H], Rv[:, kb(c)], T.pr[:, qb(c)], start=(c == 0), stop=(c == KB - 1)
                      ).then_inc(S.rod, 1)

        def down(c):
            dve.wait_ge(S["rt%d" % c], 1)
            dve.tensor_copy(T.pr[:, qb(c)], B[c][:, 128:128 + QP]).then_inc(S["rc%d" % c], 1)

        turn(0)
        turn(1)
        if own_kv:
            pe.wait_ge(S.ldv, 16)
        else:
            pe.wait_ge(S.vxa, nw)
        vsum(0)
        turn(2)
        vsum(1)
        turn(3)
        vsum(2)
        vsum(3)
        down(0)
        down(1)
        down(2)
        for c in range(KB):
            dve.wait_ge(S["re%d" % c], 1)
        dve.tensor_reduce(lsum, lp, X_, A.add).then_inc(S.rld, 1)
        down(3)
        dve.wait_ge(S.rld, 1)
        dve.tensor_copy(T.msg[H, QP + 1:QP + 2], lsum).then_inc(S.rl2d, 1)
        dve.wait_ge(S.rod, KB)
        dve.tensor_copy(T.msg[:, H], T.bo[:, H]).then_inc(S.rfd, 1)

        if not own_q:
            for s in (S.msd, S.rgd, S.rl2d, S.rfd):
                g.wait_ge(s, 1)
            send(cores[edge + 1], T.land[:, 0:MW], T.msg[:, 0:MW], S.parr)
    if sent[0]:
        g.wait_ge(S.sent, sent[0])

    pe.wait_ge(S.led, 1)
    for c in range(KB):
        pe.matmul(T.bl[:, qb(c)], T.pta[H, kb(c)], T.idn[H, H], start=True, stop=True).then_inc(S.ltd, 1)
    dve.wait_ge(S.ltd, KB)
    dve.tensor_copy(T.pa[:], T.bl[:, 0:KB * QP]).then_inc(S.lcd, 1)
    pe.wait_ge(S.lcd, 1)
    pe.wait_ge(S.ldv, 16)
    ob = T.bl[H, KB * QP:KB * QP + 128]
    for c in range(KB):
        pe.matmul(ob, T.pa[:, qb(c)], T.vs[:, kb(c)], start=(c == 0), stop=(c == KB - 1)).then_inc(S.lod, 1)
    dve.wait_ge(S.lod, KB)
    dve.wait_ge(S.led, 1)

    if not has_prev:
        dve.reciprocal(rc, la).then_inc(S.crd, 1)
        dve.wait_ge(S.crd, 1)
        dve.tensor_scalar(T.ys[H, :], ob, rc, None, A.mult).then_inc(S.cyd, 2)
    else:
        dve.tensor_copy(T.oa[H, :], ob).then_inc(S.locd, 1)
        part = T.land if asks else T.msg

        def there(qu):
            if asks:
                qu.wait_ge(S.parr, NE)
            else:
                for s in (S.rgd, S.rl2d, S.rfd):
                    qu.wait_ge(s, 1)

        there(pe)
        pe.matmul(T.bc[H, H], part[:, H], T.idn[:, 0:QP], start=True, stop=False).then_inc(S.cmd, 1)
        pe.matmul(T.b0[H, H], part[:, H], T.idn[:, QP:128], start=True, stop=False).then_inc(S.cmd, 1)
        there(dve)
        dve.wait_ge(S.lmd, 1)
        dve.tensor_scalar(dc, part[H, QP:QP + 1], na, 60.0, A.subtract, A.min).then_inc(S.cdd, 1)
        dve.tensor_copy(lb, part[H, QP + 1:QP + 2]).then_inc(S.cbd, 1)
        act.wait_ge(S.cdd, 1)
        act.activation(ec, dc, F.Exp).then_inc(S.ced, 1)
        act.wait_ge(S.ced, 1)
        act.wait_ge(S.idd, 1)
        act.activation(T.dg[H, :], T.idn[H, H], F.Copy, scale=ec).then_inc(S.cgd, 1)
        pe.wait_ge(S.cgd, 1)
        pe.wait_ge(S.locd, 1)
        pe.matmul(T.bc[H, H], T.dg[H, :], T.oa[H, 0:QP], start=False, stop=True).then_inc(S.cmd, 1)
        pe.matmul(T.b0[H, H], T.dg[H, :], T.oa[H, QP:128], start=False, stop=True).then_inc(S.cmd, 1)
        dve.wait_ge(S.ced, 1)
        dve.wait_ge(S.cbd, 1)
        dve.tensor_scalar(lc, la, ec, lb, A.mult, A.add).then_inc(S.cld, 1)
        dve.wait_ge(S.cld, 1)
        dve.reciprocal(rc, lc).then_inc(S.crd, 1)
        dve.wait_ge(S.crd, 1)
        dve.wait_ge(S.cmd, 4)
        dve.tensor_scalar(T.ys[H, 0:QP], T.bc[H, H], rc, None, A.mult).then_inc(S.cyd, 1)
        act.wait_ge(S.crd, 1)
        act.wait_ge(S.cmd, 4)
        act.activation(T.ys[H, QP:128], T.b0[H, H], F.Copy, scale=rc).then_inc(S.cyd, 1)

    sp.wait_ge(S.cyd, 2)
    sp.dma_start(T.y[:], T.ys[H, :]).then_inc(S.sty, 16)
    sp.wait_ge(S.sty, 16)
